import numpy as np
import ml_dtypes


def mxq(x, axis, fmt="e4m3"):
    dtype, down = {"e4m3": (ml_dtypes.float8_e4m3fn, 7), "e5m2": (ml_dtypes.float8_e5m2, 14)}[fmt]
    v = np.moveaxis(np.asarray(x, np.float32).astype(ml_dtypes.bfloat16).astype(np.float64), axis, -1)
    blocks = v.reshape(v.shape[:-1] + (-1, 32))
    amax = np.abs(blocks).max(-1, keepdims=True)
    byte = np.maximum(np.where(amax > 0, np.frexp(amax)[1] - 1 + 127, 0) - down, 1)
    scale = np.exp2(byte - 127.0)
    codes = (blocks / scale).astype(np.float32).astype(dtype).astype(np.float64)
    return np.moveaxis((codes * scale).reshape(v.shape), -1, axis)


WIDE = False


def mx_kscale(k):
    if not WIDE:
        return np.ones(k)
    levels = np.array([10, -10, 5, -5, 0])
    if k % 512:
        return np.exp2(np.random.permutation(np.resize(levels, k // 32))).repeat(32)
    a = np.empty((k // 512, 16))
    for p in range(k // 512):
        a[p, :8] = np.random.permutation(np.resize(levels, 8))
        for g in range(8):
            far = levels[np.abs(levels - a[p, g]) >= 10]
            a[p, g + 8] = far[np.random.randint(len(far))]
    return np.exp2(a.ravel()).repeat(32)


def f64(x):
    return np.asarray(x).astype(np.float64)


def striped(idx):
    return np.tile(idx.reshape(-1, 16).T, (8, 1)).astype(np.uint16)


def unstriped(offs):
    return offs[:16].T.reshape(-1).astype(np.int64)


def striped8(idx):
    return np.concatenate([x.reshape(-1, 16).T for x in idx]).astype(np.uint16)


def runs(offs, k):
    lists = np.stack([offs[16 * r : 16 * r + 16].T.reshape(-1) for r in range(8)]).astype(np.int64)
    return lists[np.arange(k) % 512 // 64]


def pack_weight(w):
    k, n = w.shape
    w = f64(np.asarray(w, np.float32).astype(ml_dtypes.bfloat16)).reshape(k // 32, 32, n)
    amax = np.abs(w).max(1)
    byte = np.clip(np.where(amax > 0, np.frexp(amax)[1] - 1 + 127 - 7, 1), 1, 254)
    scaled = (w * np.exp2(127.0 - byte)[:, None, :]).reshape(k, n).astype(np.float32)
    words = np.ascontiguousarray(scaled.reshape(k // 512, 128, 4, n).transpose(0, 1, 3, 2)).astype(ml_dtypes.float8_e4m3fn).view(np.uint8)
    return words, np.ascontiguousarray(byte.astype(np.uint8).reshape(k // 512, 16, n))


def unpack_weight(words, scales):
    g, p, n, _ = words.shape
    vals = np.ascontiguousarray(words).view(ml_dtypes.float8_e4m3fn).astype(np.float64) * np.repeat(np.exp2(scales.astype(np.float64) - 127.0), 8, axis=1)[..., None]
    return vals.transpose(0, 1, 3, 2).reshape(g * 512, n)


def sigmoid(v):
    return 1.0 / (1.0 + np.exp(-np.maximum(v, -700.0)))


K, T, S, N, G, H, W = 512, 1024, 512, 512, 2048, 512, 256


def setup_inputs():
    n = np.random.standard_normal
    s = mx_kscale(K)[:, None]
    u = mx_kscale(S)
    packed_xT = pack_weight(n((K, T)) * s)
    packed_dT = pack_weight(n((K, G)) / s)
    perm = np.random.permutation(S)
    return {
        "x_words": packed_xT[0],
        "x_scales": packed_xT[1],
        "d_words": packed_dT[0],
        "d_scales": packed_dT[1],
        "gn": (np.random.uniform(0.5, 1.5, (H, 1)) * u[:, None]).astype(np.float32),
        "w1": (n((H, N)) / np.sqrt(H) / u[:, None]).astype(np.float32),
        "sl": np.random.uniform(1.0, 2.0, (N, 1)).astype(np.float32),
        "th": (0.5 * n((N, 1))).astype(np.float32),
        "offs": striped(np.random.permutation(T)[:S]),
        "k1": striped8(np.random.randint(0, G, (8, H))),
        "two": striped(np.random.permutation(T)[:S]),
        "k2": striped8(np.random.randint(0, G, (8, H))),
        "n1": striped8(np.stack([np.random.permutation(S) for _ in range(8)])),
        "n2": striped8(np.stack([np.random.permutation(S) for _ in range(8)])),
        "n3": striped(perm[:W]),
        "n4": striped(perm[W:]),
    }


def reference(x_words, x_scales, d_words, d_scales, gn, w1, sl, th, offs, k1, two, k2, n1, n2, n3, n4):
    d_k1 = unpack_weight(d_words, d_scales)[np.arange(K)[:, None], runs(k1, K)]
    xq = unpack_weight(x_words, x_scales)[:, unstriped(offs)]
    a = 0.0625 * (d_k1.T @ xq)
    d_k2 = unpack_weight(d_words, d_scales)[np.arange(K)[:, None], runs(k2, K)]
    x_two = unpack_weight(x_words, x_scales)[:, unstriped(two)]
    b = 0.0625 * (d_k2.T @ x_two)
    z = f64(gn) * (a + (sigmoid(b[np.arange(H)[:, None], runs(n2, H)] - b)) * (a[np.arange(H)[:, None], runs(n1, H)] - a))
    h = mxq(f64(w1), 0, "e4m3").T @ mxq(z, 0, "e4m3")
    pb = h[:, unstriped(n4)]
    sg = sigmoid(f64(sl) * (h[:, unstriped(n3)] - f64(th)))
    rb = pb - sg
    pa = h[:, unstriped(n3)]
    sg2 = sigmoid(f64(sl) * (h[:, unstriped(n4)] - f64(th)))
    ra = pa * sg2
    ds = np.zeros((N, S))
    ds[:, unstriped(n3)] = ra
    out = ds.copy()
    out[:, unstriped(n4)] = rb
    return out

from contextlib import ExitStack

import concourse.mybir as mybir

K, T, S, N, G, H, W = 512, 1024, 512, 512, 2048, 512, 256
FLOPS = 3 * 2 * 512 * 512 * 512

F32 = mybir.dt.float32
BF16 = mybir.dt.bfloat16
I32 = mybir.dt.int32
U32 = mybir.dt.uint32
U16 = mybir.dt.uint16
U8 = mybir.dt.uint8
FP8X4 = mybir.dt.float8_e4m3fn_x4
ALU = mybir.AluOpType
ACT = mybir.ActivationFunctionType

P = 128
PACK = 4
HALF = S // 2
LIST_COLS = HALF // 16


def tile_picked_twpqpullbeod_none_p_kernel(
    tc, x_words, x_scales, d_words, d_scales, gn, w1, sl, th, offs, k1, two, k2, n1, n2, n3, n4, out
):
    nc = tc.nc
    with ExitStack() as ctx:
        keep = ctx.enter_context(tc.tile_pool(name="keep", bufs=1))
        stage = ctx.enter_context(tc.tile_pool(name="stage", bufs=1))
        psum = ctx.enter_context(tc.psum_pool(name="psum", bufs=1))

        def tile(shape, dtype, name):
            return keep.tile(shape, dtype, name=name, align_bytes=64)

        def staged(shape, dtype, name, offset):
            if offset is None:
                return tile(shape, dtype, name)
            return stage.tile(shape, dtype, name=name, align_bytes=64, offset=offset)

        def load_list(src, name):
            lst = tile(list(src.shape), U16, name)
            nc.sync.dma_start(lst[:], src)
            return lst

        d_bytes = tile([P, G], U8, "d_bytes")
        x_bytes = tile([P, T], U8, "x_bytes")
        nc.gpsimd.memset(d_bytes[:].bitcast(I32), 0)
        nc.vector.memset(x_bytes[:].bitcast(I32), 0)

        nc.gpsimd.dma_start(d_bytes[0:P:8, :].bitcast(I32), d_scales[0].bitcast(I32))
        two_l = load_list(two, "two_l")
        x_tab = tile([P, T], U32, "x_tab")
        nc.sync.dma_start(x_tab[:].bitcast(I32), x_words[0].rearrange("p n t -> p (n t)").bitcast(I32))
        k2_l = load_list(k2, "k2_l")
        k1_l = load_list(k1, "k1_l")
        offs_l = load_list(offs, "offs_l")
        n2_l = load_list(n2, "n2_l")
        d_tab = tile([P, G], U32, "d_tab")
        nc.sync.dma_start(d_tab[:].bitcast(I32), d_words[0].rearrange("p n t -> p (n t)").bitcast(I32))
        n1_l = load_list(n1, "n1_l")
        n3_l = load_list(n3, "n3_l")
        n4_l = load_list(n4, "n4_l")
        for q in range(4):
            nc.scalar.dma_start(
                x_bytes[32 * q : 32 * q + 4, :].bitcast(I32), x_scales[0, 4 * q : 4 * q + 4, :].bitcast(I32)
            )

        def coded_product(code_l, token_l, name, move_queue, at):
            x_got = staged([P, S], U32, name + "_xg", at[2])
            nc.vector.tensor_copy(x_got[:], x_tab[:].indirect(token_l[:]))
            d_bytes_got = staged([P, H], U8, name + "_dbg", at[0])
            nc.vector.tensor_copy(d_bytes_got[:], d_bytes[:].indirect(code_l[:]))
            d_plane = tile([P, H], U8, name + "_dpl")
            nc.vector.tensor_copy(
                d_plane[:].rearrange("p (t c i) -> p c t i", t=PACK, i=16),
                d_bytes_got[:].rearrange("p (c i t) -> p c t i", t=PACK, i=16),
            )
            for r in range(1, 4):
                move_queue.dma_start(d_plane[r:P:32, :].bitcast(I32), d_plane[8 * r : P : 32, :].bitcast(I32))
            d_got = staged([P, H], U32, name + "_dg", at[3])
            nc.vector.tensor_copy(d_got[:], d_tab[:].indirect(code_l[:]))
            d_dealt = tile([P, H], U32, name + "_dd")
            nc.vector.tensor_copy(
                d_dealt[:].bitcast(I32).rearrange("p (t c i) -> p c t i", t=PACK, i=4),
                d_got[:].bitcast(I32).rearrange("p (c i t) -> p c t i", t=PACK, i=4),
            )
            x_plane = staged([P, S], U8, name + "_xpl", at[1])
            nc.vector.tensor_copy(x_plane[:], x_bytes[:].indirect(token_l[:]))
            banks = []
            for t in range(PACK):
                bank = psum.tile([P, S], F32, name="%s_bank%d" % (name, t), tag="%s_bank%d" % (name, t))
                cols = slice(P * t, P * (t + 1))
                nc.tensor.matmul_mx(
                    out=bank[:],
                    lhsT=d_dealt[:, cols].bitcast(FP8X4),
                    lhsT_scale=d_plane[:, cols],
                    rhs=x_got[:].bitcast(FP8X4),
                    rhs_scale=x_plane[:],
                    start=True,
                    stop=True,
                )
                banks.append(bank)
            return banks

        b_banks = coded_product(k2_l, two_l, "b", nc.scalar, (13312, None, 5120, 1536))
        w_raw = staged([P, PACK, N], F32, "w_raw", 13312)
        nc.sync.dma_start(w_raw[:], w1.rearrange("(p j) n -> p j n", j=PACK))
        a_banks = coded_product(k1_l, offs_l, "a", nc.sync, (2048, 2560, 3072, 0))

        gain = staged([P, PACK], F32, "gain", 5120)
        nc.sync.dma_start(gain[:], gn.rearrange("(p t) o -> p (t o)", t=PACK))
        slope = staged([P, PACK], F32, "slope", 5184)
        thresh = staged([P, PACK], F32, "thresh", 5248)
        with nc.allow_non_contiguous_dma(reason="one value a row of h"):
            nc.sync.dma_start(slope[:], sl.rearrange("(t p) o -> p (t o)", p=P))
            nc.sync.dma_start(thresh[:], th.rearrange("(t p) o -> p (t o)", p=P))
        w_bf = tile([P, N, PACK], BF16, "w_bf")
        for c in range(4):
            cols = slice(P * c, P * (c + 1))
            nc.gpsimd.tensor_scalar(
                w_bf[:, cols, :], w_raw[:, :, cols].rearrange("p j n -> p n j"), 1.0, 0.0, ALU.mult, ALU.add
            )

        halves = [slice(HALF * u, HALF * (u + 1)) for u in range(2)]
        list_halves = [slice(LIST_COLS * u, LIST_COLS * (u + 1)) for u in range(2)]

        diffs = []
        for t in range(PACK):
            b_row = tile([P, S], F32, "b_row%d" % t)
            nc.scalar.copy(b_row[:], b_banks[t][:])
            b_got = tile([P, S], F32, "b_got%d" % t)
            for u in range(2):
                nc.scalar.activation(b_got[:, halves[u]], b_row[:].indirect(n2_l[:, list_halves[u]]), ACT.Copy)
            diff = tile([P, S], F32, "diff%d" % t)
            nc.gpsimd.tensor_tensor(diff[:], b_got[:], b_row[:], ALU.subtract)
            diffs.append(diff)

        w_codes = tile([P, N], U32, "w_codes")
        w_plane = tile([P, N], U8, "w_plane")
        nc.vector.quantize_mx(
            out=w_codes[:].bitcast(FP8X4), scales=w_plane[:], in_=w_bf[:].rearrange("p n j -> p (n j)")
        )

        gain16 = tile([P, PACK], F32, "gain16")
        nc.vector.tensor_scalar(gain16[:], gain[:], 0.0625, None, ALU.mult)

        gate = tile([P, PACK, S], F32, "gate")
        a_rows = []
        for t in range(PACK):
            nc.scalar.activation(gate[:, t, :], diffs[t][:], ACT.Sigmoid, scale=0.0625)
            a_row = tile([P, S], F32, "a_row%d" % t)
            if t < 3:
                nc.vector.tensor_scalar(a_row[:], a_banks[t][:], gain16[:, t : t + 1], None, ALU.mult)
            else:
                nc.scalar.activation(a_row[:], a_banks[t][:], ACT.Copy, scale=gain16[:, t : t + 1])
            a_rows.append(a_row)

        bias = tile([P, PACK], F32, "bias")
        nc.vector.scalar_tensor_tensor(bias[:], slope[:], -1.0, thresh[:], ALU.mult, ALU.mult)
        stay = tile([P, PACK, S], F32, "stay")
        for t in range(PACK):
            nc.vector.scalar_tensor_tensor(stay[:, t, :], gate[:, t, :], 1.0, a_rows[t][:], ALU.subtract, ALU.mult)

        h_banks = [
            [psum.tile([P, HALF], F32, name="h_bank%d%d" % (u, m), tag="%s_bank%d" % ("ba"[u], m)) for m in range(PACK)]
            for u in range(2)
        ]
        h_rows = [tile([P, S], F32, "h_row%d" % m) for m in range(PACK)]
        for u in range(2):
            a_got = tile([P, PACK, HALF], F32, "a_got%d" % u)
            pull = tile([P, PACK, HALF], F32, "pull%d" % u)
            for t in range(PACK):
                nc.scalar.activation(a_got[:, t, :], a_rows[t][:].indirect(n1_l[:, list_halves[u]]), ACT.Copy)
                nc.vector.tensor_tensor(pull[:, t, :], a_got[:, t, :], gate[:, t, halves[u]], ALU.mult)
            z_bf = tile([P, HALF, PACK], BF16, "z_bf%d" % u)
            nc.vector.tensor_tensor(
                z_bf[:].rearrange("p (c i) t -> p c t i", i=4),
                pull[:].rearrange("p t (c i) -> p c t i", i=4),
                stay[:, :, halves[u]].rearrange("p t (c i) -> p c t i", i=4),
                ALU.subtract,
            )
            z_codes = tile([P, HALF], U32, "z_codes%d" % u)
            z_plane = tile([P, HALF], U8, "z_plane%d" % u)
            nc.vector.quantize_mx(
                out=z_codes[:].bitcast(FP8X4), scales=z_plane[:], in_=z_bf[:].rearrange("p n j -> p (n j)")
            )
            for m in range(PACK):
                cols = slice(P * m, P * (m + 1))
                nc.tensor.matmul_mx(
                    out=h_banks[u][m][:],
                    lhsT=w_codes[:, cols].bitcast(FP8X4),
                    lhsT_scale=w_plane[:, cols],
                    rhs=z_codes[:].bitcast(FP8X4),
                    rhs_scale=z_plane[:],
                    start=True,
                    stop=True,
                )

        for m in range(PACK):
            nc.scalar.copy(h_rows[m][:, halves[0]], h_banks[0][m][:])
            nc.vector.tensor_copy(h_rows[m][:, halves[1]], h_banks[1][m][:])

        out_rows = [tile([P, S], F32, "out_row%d" % m) for m in range(PACK)]
        ras, rbs = [], []

        def put_a(m):
            nc.scalar.activation(out_rows[m][:].indirect(n3_l[:]), ras[m][:], ACT.Copy)

        def put_b(m):
            nc.scalar.activation(out_rows[m][:].indirect(n4_l[:]), rbs[m][:], ACT.Copy)
            nc.sync.dma_start(out[P * m : P * (m + 1), :], out_rows[m][:])

        for m in range(PACK):
            col = slice(m, m + 1)
            pa = tile([P, W], F32, "pa%d" % m)
            sg2 = tile([P, W], F32, "sg2%d" % m)
            pb = tile([P, W], F32, "pb%d" % m)
            sg = tile([P, W], F32, "sg%d" % m)
            ra = tile([P, W], F32, "ra%d" % m)
            rb = tile([P, W], F32, "rb%d" % m)
            nc.scalar.activation(pa[:], h_rows[m][:].indirect(n3_l[:]), ACT.Copy)
            nc.scalar.activation(
                sg2[:], h_rows[m][:].indirect(n4_l[:]), ACT.Sigmoid, bias=bias[:, col], scale=slope[:, col]
            )
            nc.vector.tensor_tensor(ra[:], pa[:], sg2[:], ALU.mult)
            ras.append(ra)
            if m > 0:
                put_b(m - 1)
            nc.scalar.activation(pb[:], h_rows[m][:].indirect(n4_l[:]), ACT.Copy)
            nc.scalar.activation(
                sg[:], h_rows[m][:].indirect(n3_l[:]), ACT.Sigmoid, bias=bias[:, col], scale=slope[:, col]
            )
            nc.vector.tensor_tensor(rb[:], pb[:], sg[:], ALU.subtract)
            rbs.append(rb)
            put_a(m)
        put_b(PACK - 1)
